import numpy as np, ml_dtypes
CORES = [120,124,248,252,376,380,504,508]
N = 8
NH, QP = 8, 128
def setup_inputs(rng):
    q = rng.standard_normal((N, 128, NH * QP), dtype=np.float32) / 4; k = rng.standard_normal((N, 128, NH * 128), dtype=np.float32)
    a = 2 * np.pi * rng.random((N, NH * QP)); s = 400 * rng.random((N, NH * QP)) ** 1.5; q[:, 0, :] = s * np.cos(a); q[:, 1, :] = s * np.sin(a); q[:, 2, :] = 150 * rng.standard_normal((N, NH * QP)); k[:, 2, :] = 1 + k[:, 2, :] / 50
    a = (2 * np.pi * rng.random((1, NH, 1)) + np.pi / 2 * (rng.permuted(np.tile(np.arange(N), (NH, 1)), axis=1).T.reshape(N, NH, 1) + 0.5) / N - 0.5 + rng.random((N, NH, 128))).reshape(N, NH * 128); k[:, 0, :] = np.cos(a); k[:, 1, :] = np.sin(a)
    return {"q": q.astype(ml_dtypes.bfloat16), "k": k.astype(ml_dtypes.bfloat16), "v": rng.standard_normal((N, 128, NH * 128), dtype=np.float32).astype(ml_dtypes.bfloat16)}
def setup_inputs_big(rng):
    d = setup_inputs(rng)
    for k in ("v",): d[k] = (d[k].astype(np.float32) * 1048576.0).astype(d[k].dtype)
    return d
def setup_inputs_small(rng):
    d = setup_inputs(rng)
    for k in ("v",): d[k] = (d[k].astype(np.float32) * (1 / 1048576.0)).astype(d[k].dtype)
    return d
def reference(q, k, v):
    Q, K, V = q.astype(np.float64), k.astype(np.float64), v.astype(np.float64)
    y = np.zeros((N, QP, NH * 128))
    for r in range(N):
        for h in range(NH):
            S = np.concatenate([K[j][:, 128 * h:128 * h + 128].T @ Q[r][:, QP * h:QP * h + QP] for j in range(N)], axis=0)
            P = np.exp(S - S.max(axis=0)); P = P / P.sum(axis=0)
            y[r][:, 128 * h:128 * h + 128] = P.T @ np.concatenate([V[j][:, 128 * h:128 * h + 128] for j in range(N)], axis=0)
    return {"y": y.astype(ml_dtypes.bfloat16)}

@@ -1,0 +1,287 @@
+from concourse.bass import DstId, RemoteDMATransfer
+from concourse.mybir import AluOpType, AxisListType, ActivationFunctionType
+
+NSIM = 512
+D = 128
+PK = 3 * D
+NEV = 84
+
+SCRATCH = {
+    "ql": ("sbuf", [128, 1024], "bfloat16"), "kl": ("sbuf", [128, 1024], "bfloat16"),
+    "vl": ("sbuf", [128, 1024], "bfloat16"),
+    "x": ("sbuf", [128, 8 * PK], "bfloat16"),
+    "own": ("sbuf", [128, 2 * PK], "bfloat16"),
+    "kv": ("sbuf", [128, 4 * 512], "bfloat16"),
+    "rl": ("sbuf", [128, PK], "bfloat16"), "rl2": ("sbuf", [128, D], "bfloat16"),
+    "p": ("sbuf", [128, 8 * 256], "bfloat16"), "pts": ("sbuf", [128, 8 * 256], "bfloat16"),
+    "oo": ("sbuf", [128, 8 * D], "bfloat16"),
+    "st": ("sbuf", [128, 64], "float32"),
+    "yo": ("sbuf", [128, 2 * D], "bfloat16"), "yl": ("sbuf", [128, 1024], "bfloat16"),
+    "ones": ("sbuf", [128, D], "bfloat16"), "idn": ("sbuf", [128, D], "bfloat16"),
+    "s00": ("psum", [128, 512], "float32"), "s01": ("psum", [128, 512], "float32"),
+    "s10": ("psum", [128, 512], "float32"), "s11": ("psum", [128, 512], "float32"),
+    "pt0": ("psum", [128, 1024], "bfloat16"), "pt1": ("psum", [128, 1024], "bfloat16"),
+    "o0": ("psum", [128, 512], "float32"), "o1": ("psum", [128, 512], "float32"),
+}
+SEMAPHORES = (["ld", "st", "snt", "own", "rl", "rl2", "rpd", "rpx", "rpo", "rpc", "rps"]
+              + ["kv%d" % i for i in range(4)] + ["ya%d" % i for i in range(4)] + ["e%d" % i for i in range(NEV)])
+
+IDX = {"own": 0, "dg": 1, "sw": 2, "cb": 3}
+DUE = ["own", "dg", "cb", "sw"]
+
+
+def _bits(m):
+    return [i for i in range(m.bit_length()) if (m >> i) & 1]
+
+
+def _mask(lst):
+    return sum(1 << i for i in lst)
+
+
+def rank_program(g, core, T, topo):
+    cores = [int(c) for c in T.cores]
+    if not any(topo.host(c) == topo.host(core) and topo.chip(c) == topo.chip(core) for c in cores):
+        return
+    hosts = []
+    for c in cores:
+        if topo.host(c) not in hosts:
+            hosts.append(topo.host(c))
+    ranks_of = {H: [r for r, c in enumerate(cores) if topo.host(c) == H] for H in hosts}
+
+    def kind(A, B):
+        a, b = cores[ranks_of[A][0]], cores[ranks_of[B][0]]
+        if A == B:
+            return "own"
+        if not topo.may_write(a, b):
+            return "dg"
+        return "sw" if topo.same_plane(a, b) else "cb"
+    nb = {A: {kind(A, B): B for B in hosts} for A in hosts}
+    group = {}
+    for h, c in enumerate(cores):
+        group[h] = [c] + sorted(x for x in range(NSIM) if x != c and topo.host(x) == topo.host(c)
+                                and topo.chip(x) == topo.chip(c) and topo.die(x) == topo.die(c))
+
+    def head_on(H, die):
+        return [h for h in ranks_of[H] if topo.die(cores[h]) == die][0]
+
+    head = [h for h in group if core in group[h]][0]
+    idx = group[head].index(core)
+    C = topo.host(core)
+    mykind = [k for k in IDX if IDX[k] == idx][0]
+    src_host = nb[C][mykind]
+    sr = ranks_of[src_host]
+    sibs = [x for x in group[head] if x != core]
+
+    m_on = topo.mask(core, sibs[0])
+    m_off = topo.mask(core, cores[ranks_of[nb[C]["sw"]][0]])
+    offb = _bits(m_off)
+    half = [_mask(offb[:len(offb) // 2]), _mask(offb[len(offb) // 2:])]
+    m_up = m_on & ~m_off
+    cnt = lambda m: len(_bits(m))
+
+    te, ve, ac, sy, sem = g.tensor, g.vector, g.scalar, g.sync, T.sem
+    nev, sent = [0], [0]
+
+    def ev():
+        nev[0] += 1
+        return sem["e%d" % (nev[0] - 1)]
+
+    def tr(src, dst, dests, mask, rsem):
+        ids = []
+        for d in dests:
+            rid, pid = topo.addr(d, core)
+            ids.append(DstId(rid=rid, pnc=pid))
+        sent[0] += cnt(mask)
+        if len(dests) == 1:
+            return RemoteDMATransfer(dst_ids=ids, dma_engine_mask=mask, remote_sem=rsem, src=src, dst=dst)
+        return RemoteDMATransfer(dst_ids=ids, dma_engine_mask=mask, remote_sem=rsem, srcs=[src],
+                                 dsts=[dst for _ in dests])
+
+    def send(trs):
+        g.remote_dma_fused(trs, local_sem=sem.snt)
+
+    eone, eidn = ev(), ev()
+    ve.memset(T.ones[:], 1.0).then_inc(eone, 1)
+    g.wait_ge(eone, 1)
+    g.affine_select(T.idn[:], T.ones[:], [[-1, D]], AluOpType.is_equal, 0.0, 0, 1).then_inc(eidn, 1)
+
+    own_waits = [(sem.own, {0: cnt(m_up), 1: 2 * cnt(m_off), 2: 2 * cnt(half[0]), 3: 2 * cnt(half[0])}[idx])]
+    myb, other = 0, 0
+    if idx == 0:
+        myb = ranks_of[C].index(head)
+        other = [h for h in ranks_of[C] if h != head][0]
+        sy.dma_start(T.ql[:], T.q[:]).then_inc(sem.ld, 16)
+        ac.dma_start(T.kl[:], T.k[:]).then_inc(sem.ld, 16)
+        sy.dma_start(T.vl[:], T.v[:]).then_inc(sem.ld, 16)
+        ve.wait_ge(sem.ld, 48)
+        oq, ok = (0, 2 * D) if myb == 0 else (2 * D, 0)
+
+        def pack(h, out, o0, s):
+            for buf, off in ((T.ql, oq), (T.vl, D), (T.kl, ok)):
+                ve.tensor_copy(out[:, o0 + off:o0 + off + D], buf[:, h * D:(h + 1) * D]).then_inc(s, 1)
+        for h in ranks_of[nb[C]["dg"]]:
+            pack(h, T.x, h * PK, sem.rpd)
+        pack(other, T.x, other * PK, sem.rpx)
+        pack(head, T.own, myb * PK, sem.rpo)
+        for h in ranks_of[nb[C]["cb"]]:
+            pack(h, T.x, h * PK, sem.rpc)
+        for h in ranks_of[nb[C]["sw"]]:
+            pack(h, T.x, h * PK, sem.rps)
+        own_waits.append((sem.rpo, 3))
+
+        land = T.own[:, myb * PK:(myb + 1) * PK]
+        pk = lambda h: T.x[:, h * PK:(h + 1) * PK]
+        relg = group[head_on(nb[C]["sw"], topo.die(core))]
+        g.wait_ge(sem.rpd, 6)
+        send([tr(pk(h), T.rl[:], [relg[2 + i]], half[i], sem.rl) for i, h in enumerate(ranks_of[nb[C]["dg"]])])
+        g.wait_ge(sem.rpx, 3)
+        send([tr(pk(other), land, [cores[other]], m_up, sem.own)])
+        for kd, s in (("cb", sem.rpc), ("sw", sem.rps)):
+            g.wait_ge(s, 6)
+            send([tr(pk(h), land, [group[h][IDX[kind(nb[C][kd], C)]]], half[i], sem.own)
+                  for i, h in enumerate(ranks_of[nb[C][kd]])])
+    elif idx >= 2:
+        A = nb[C]["sw"]
+        rr = head_on(A, topo.die(core))
+        hh = ranks_of[nb[A]["dg"]][idx - 2]
+        bb = ranks_of[A].index(rr)
+        g.wait_ge(sem.rl, cnt(half[0]))
+        send([tr(T.rl[:], T.own[:, bb * PK:(bb + 1) * PK], [group[hh][IDX["dg"]]], m_off, sem.own)])
+
+    m_fw = m_up if idx == 0 else m_on
+    for s, v in own_waits:
+        g.wait_ge(s, v)
+    slot = hosts.index(src_host)
+    send([tr(T.own[:, D:D + 512], T.kv[:, slot * 512:(slot + 1) * 512], sibs, m_fw, sem["kv%d" % slot])])
+
+    S = [[T.s00, T.s01], [T.s10, T.s11]]
+    PT, O = [T.pt0, T.pt1], [T.o0, T.o1]
+    q = [T.own[:, 0:D], T.own[:, 5 * D:6 * D]]
+    stc = lambda gi, j: T.st[:, gi * 14 + 2 * j:gi * 14 + 2 * j + 2]
+    nmg = lambda gi: stc(gi, 0)
+    nm = lambda gi: stc(gi, 0) if gi == 0 else stc(gi, 1)
+    dd, al, lg, tmp = (lambda gi: stc(gi, 2)), (lambda gi: stc(gi, 3)), (lambda gi: stc(gi, 4)), (lambda gi: stc(gi, 5))
+    ll = lambda gi: stc(gi, 4) if gi == 0 else stc(gi, 6)
+    rc = T.st[:, 56:58]
+    blk = lambda buf, gi, b, w: buf[:, (gi * 2 + b) * w:(gi * 2 + b + 1) * w]
+    Exp = ActivationFunctionType.Exp
+
+    order = [mykind] + [k for k in DUE if k != mykind]
+    te.wait_ge(eidn, 1)
+    eo_prev, l_ready = None, None
+    for gi, kd in enumerate(order):
+        if gi == 0:
+            buf, c0 = T.own, D
+            for s, v in own_waits:
+                te.wait_ge(s, v)
+        else:
+            sl = hosts.index(nb[C][kd])
+            buf, c0 = T.kv, sl * 512
+            te.wait_ge(sem["kv%d" % sl], cnt(m_up) if kd == "own" else cnt(m_on))
+        kk = buf[:, c0 + D:c0 + 3 * D]
+        vv = [buf[:, c0:c0 + D], buf[:, c0 + 3 * D:c0 + 4 * D]]
+        Sg = [S[gi % 2][b][:, 0:256] for b in (0, 1)]
+        es, ered, ep, et, ec, eo = [ev(), ev()], ev(), [ev(), ev()], [ev(), ev()], [ev(), ev()], [ev(), ev()]
+        for b in (0, 1):
+            te.matmul(Sg[b], q[b], kk, True, True).then_inc(es[b], 1)
+        for b in (0, 1):
+            ve.wait_ge(es[b], 1)
+            ve.tensor_reduce(nmg(gi)[:, b:b + 1], Sg[b], AxisListType.X, AluOpType.max, negate=True).then_inc(ered, 1)
+        ve.wait_ge(ered, 2)
+        if gi > 0:
+            enm, ed, eal, ers = ev(), ev(), ev(), [ev(), ev()]
+            ve.tensor_tensor(nm(gi), nm(gi - 1), nmg(gi), AluOpType.min).then_inc(enm, 1)
+            ve.wait_ge(enm, 1)
+            ve.tensor_tensor(dd(gi), nm(gi), nm(gi - 1), AluOpType.subtract).then_inc(ed, 1)
+            ac.wait_ge(enm, 1)
+        else:
+            ac.wait_ge(ered, 2)
+        ac.activation(blk(T.p, gi, 0, 256), Sg[0], Exp, bias=nm(gi)[:, 0:1], scale=1.0,
+                      accum_out=lg(gi)[:, 0:1]).then_inc(ep[0], 1)
+        if gi > 0:
+            ac.wait_ge(ed, 1)
+            ac.activation(al(gi), dd(gi), Exp).then_inc(eal, 1)
+        ac.activation(blk(T.p, gi, 1, 256), Sg[1], Exp, bias=nm(gi)[:, 1:2], scale=1.0,
+                      accum_out=lg(gi)[:, 1:2]).then_inc(ep[1], 1)
+        if gi > 0:
+            ve.wait_ge(eal, 1)
+            for b in (0, 1):
+                ve.wait_ge(eo_prev[b][0], eo_prev[b][1])
+                ve.tensor_scalar(blk(T.oo, gi, b, D), O[b][:, 0:D], al(gi)[:, b:b + 1], None,
+                                 AluOpType.mult).then_inc(ers[b], 1)
+        for b in (0, 1):
+            te.wait_ge(ep[b], 1)
+            for j in (0, 1):
+                te.transpose(PT[b][:, j * D:(j + 1) * D], blk(T.p, gi, b, 256)[:, j * D:(j + 1) * D],
+                             T.idn[:]).then_inc(et[b], 1)
+            if gi > 0:
+                te.wait_ge(ers[b], 1)
+                te.matmul(O[b][:, 0:D], T.idn[:], blk(T.oo, gi, b, D), True, False).then_inc(eo[b], 1)
+        for b in (0, 1):
+            ve.wait_ge(et[b], 2)
+            ve.tensor_copy(blk(T.pts, gi, b, 256), PT[b][:, 0:256]).then_inc(ec[b], 1)
+        for b in (0, 1):
+            te.wait_ge(ec[b], 1)
+            te.matmul(O[b][:, 0:D], blk(T.pts, gi, b, 256)[:, 0:D], vv[0], gi == 0, False).then_inc(eo[b], 1)
+            te.matmul(O[b][:, 0:D], blk(T.pts, gi, b, 256)[:, D:2 * D], vv[1], False, True).then_inc(eo[b], 1)
+        eo_prev = [(eo[b], 2 if gi == 0 else 3) for b in (0, 1)]
+        if gi > 0:
+            etmp, el = ev(), ev()
+            for s, v in l_ready:
+                ve.wait_ge(s, v)
+            ve.tensor_tensor(tmp(gi), ll(gi - 1), al(gi), AluOpType.mult).then_inc(etmp, 1)
+            ve.wait_ge(etmp, 1)
+            ve.wait_ge(ep[0], 1)
+            ve.wait_ge(ep[1], 1)
+            ve.tensor_tensor(ll(gi), tmp(gi), lg(gi), AluOpType.add).then_inc(el, 1)
+            l_ready = [(el, 1)]
+        else:
+            l_ready = [(ep[0], 1), (ep[1], 1)]
+    er, ey = ev(), [ev(), ev()]
+    for s, v in l_ready:
+        ve.wait_ge(s, v)
+    ve.reciprocal(rc, ll(len(order) - 1)).then_inc(er, 1)
+    ve.wait_ge(er, 1)
+    ve.wait_ge(eo_prev[0][0], eo_prev[0][1])
+    ve.tensor_scalar(T.yo[:, 0:D], O[0][:, 0:D], rc[:, 0:1], None, AluOpType.mult).then_inc(ey[0], 1)
+    ac.wait_ge(er, 1)
+    ac.wait_ge(eo_prev[1][0], eo_prev[1][1])
+    ac.activation(T.yo[:, D:2 * D], O[1][:, 0:D], ActivationFunctionType.Identity, scale=rc[:, 1:2]).then_inc(ey[1], 1)
+
+    g.wait_ge(ey[0], 1)
+    g.wait_ge(ey[1], 1)
+    ycol = lambda h: T.yl[:, h * D:(h + 1) * D]
+    yblk = lambda i: T.yo[:, i * D:(i + 1) * D]
+    ya = sem["ya%d" % hosts.index(C)]
+    if idx == 0:
+        send([tr(yblk(1 - myb), ycol(head), [cores[other]], m_up, ya)])
+    elif idx == 1:
+        relg = group[head_on(nb[C]["sw"], topo.die(core))]
+        send([tr(yblk(i), T.rl2[:], [relg[i]], half[i], sem.rl2) for i in (0, 1)])
+    else:
+        send([tr(yblk(i), ycol(head), [cores[sr[i]]], half[i], ya) for i in (0, 1)])
+    if idx <= 1:
+        A = nb[C]["sw"]
+        hh = head_on(A, topo.die(core))
+        g.wait_ge(sem.rl2, cnt(half[0]))
+        send([tr(T.rl2[:], ycol(hh), [cores[ranks_of[nb[A]["dg"]][idx]]], m_off, sem["ya%d" % hosts.index(A)])])
+    g.wait_ge(sem.snt, sent[0])
+
+    if idx == 0:
+        nst = 1
+        sy.wait_ge(ey[0], 1)
+        sy.wait_ge(ey[1], 1)
+        sy.dma_start(T.y[:, head * D:(head + 1) * D], yblk(myb)).then_inc(sem.st, 16)
+        for kd, val in (("own", cnt(m_up)), ("cb", 2 * cnt(half[0])), ("sw", 2 * cnt(half[0])), ("dg", 2 * cnt(m_off))):
+            hs = sorted(h for h in ranks_of[nb[C][kd]] if h != head)
+            sy.wait_ge(sem["ya%d" % hosts.index(nb[C][kd])], val)
+            runs = [[hs[0], hs[0]]]
+            for h in hs[1:]:
+                if h == runs[-1][1] + 1:
+                    runs[-1][1] = h
+                else:
+                    runs.append([h, h])
+            for lo, hi in runs:
+                sy.dma_start(T.y[:, lo * D:(hi + 1) * D], T.yl[:, lo * D:(hi + 1) * D]).then_inc(sem.st, 16)
+                nst += 1
+        sy.wait_ge(sem.st, 16 * nst)

@@ -23,7 +23,7 @@ SCRATCH = {
     "pt0": ("psum", [128, 1024], "bfloat16"), "pt1": ("psum", [128, 1024], "bfloat16"),
     "o0": ("psum", [128, 512], "float32"), "o1": ("psum", [128, 512], "float32"),
 }
-SEMAPHORES = (["ld", "st", "snt", "own", "rl", "rl2", "rpd", "rpx", "rpo", "rpc", "rps"]
+SEMAPHORES = (["ld", "ld2", "st", "snt", "own", "rl", "rl2", "rpd", "rpx", "rpo", "rpc", "rps"]
               + ["kv%d" % i for i in range(4)] + ["ya%d" % i for i in range(4)] + ["e%d" % i for i in range(NEV)])
 
 IDX = {"own": 0, "dg": 1, "sw": 2, "cb": 3}
@@ -36,6 +36,16 @@ def _bits(m):
 
 def _mask(lst):
     return sum(1 << i for i in lst)
+
+
+def _runs(hs):
+    runs = [[hs[0], hs[0]]]
+    for h in hs[1:]:
+        if h == runs[-1][1] + 1:
+            runs[-1][1] = h
+        else:
+            runs.append([h, h])
+    return runs
 
 
 def rank_program(g, core, T, topo):
@@ -110,10 +120,15 @@ def rank_program(g, core, T, topo):
     if idx == 0:
         myb = ranks_of[C].index(head)
         other = [h for h in ranks_of[C] if h != head][0]
-        sy.dma_start(T.ql[:], T.q[:]).then_inc(sem.ld, 16)
-        ac.dma_start(T.kl[:], T.k[:]).then_inc(sem.ld, 16)
-        sy.dma_start(T.vl[:], T.v[:]).then_inc(sem.ld, 16)
-        ve.wait_ge(sem.ld, 48)
+        parts = [sorted(ranks_of[nb[C]["dg"]] + ranks_of[nb[C]["cb"]]), sorted(ranks_of[C] + ranks_of[nb[C]["sw"]])]
+        nld = [0, 0]
+        for pi, (hs, s) in enumerate(zip(parts, (sem.ld, sem.ld2))):
+            for lo, hi in _runs(hs):
+                for ti, (buf, t) in enumerate(((T.ql, T.q), (T.kl, T.k), (T.vl, T.v))):
+                    qu = sy if (ti + pi) % 2 == 0 else ac
+                    qu.dma_start(buf[:, lo * D:(hi + 1) * D], t[:, lo * D:(hi + 1) * D]).then_inc(s, 16)
+                    nld[pi] += 16
+        ve.wait_ge(sem.ld, nld[0])
         oq, ok = (0, 2 * D) if myb == 0 else (2 * D, 0)
 
         def pack(h, out, o0, s):
@@ -121,10 +136,11 @@ def rank_program(g, core, T, topo):
                 ve.tensor_copy(out[:, o0 + off:o0 + off + D], buf[:, h * D:(h + 1) * D]).then_inc(s, 1)
         for h in ranks_of[nb[C]["dg"]]:
             pack(h, T.x, h * PK, sem.rpd)
-        pack(other, T.x, other * PK, sem.rpx)
-        pack(head, T.own, myb * PK, sem.rpo)
         for h in ranks_of[nb[C]["cb"]]:
             pack(h, T.x, h * PK, sem.rpc)
+        ve.wait_ge(sem.ld2, nld[1])
+        pack(other, T.x, other * PK, sem.rpx)
+        pack(head, T.own, myb * PK, sem.rpo)
         for h in ranks_of[nb[C]["sw"]]:
             pack(h, T.x, h * PK, sem.rps)
         own_waits.append((sem.rpo, 3))
@@ -134,9 +150,11 @@ def rank_program(g, core, T, topo):
         relg = group[head_on(nb[C]["sw"], topo.die(core))]
         g.wait_ge(sem.rpd, 6)
         send([tr(pk(h), T.rl[:], [relg[2 + i]], half[i], sem.rl) for i, h in enumerate(ranks_of[nb[C]["dg"]])])
-        g.wait_ge(sem.rpx, 3)
-        send([tr(pk(other), land, [cores[other]], m_up, sem.own)])
-        for kd, s in (("cb", sem.rpc), ("sw", sem.rps)):
+        for kd, s in (("cb", sem.rpc), ("own", sem.rpx), ("sw", sem.rps)):
+            if kd == "own":
+                g.wait_ge(s, 3)
+                send([tr(pk(other), land, [cores[other]], m_up, sem.own)])
+                continue
             g.wait_ge(s, 6)
             send([tr(pk(h), land, [group[h][IDX[kind(nb[C][kd], C)]]], half[i], sem.own)
                   for i, h in enumerate(ranks_of[nb[C][kd]])])
@@ -154,93 +172,137 @@ def rank_program(g, core, T, topo):
     slot = hosts.index(src_host)
     send([tr(T.own[:, D:D + 512], T.kv[:, slot * 512:(slot + 1) * 512], sibs, m_fw, sem["kv%d" % slot])])
 
-    S = [[T.s00, T.s01], [T.s10, T.s11]]
+    SB = [[T.s00, T.s10], [T.s01, T.s11]]
     PT, O = [T.pt0, T.pt1], [T.o0, T.o1]
     q = [T.own[:, 0:D], T.own[:, 5 * D:6 * D]]
-    stc = lambda gi, j: T.st[:, gi * 14 + 2 * j:gi * 14 + 2 * j + 2]
-    nmg = lambda gi: stc(gi, 0)
-    nm = lambda gi: stc(gi, 0) if gi == 0 else stc(gi, 1)
-    dd, al, lg, tmp = (lambda gi: stc(gi, 2)), (lambda gi: stc(gi, 3)), (lambda gi: stc(gi, 4)), (lambda gi: stc(gi, 5))
-    ll = lambda gi: stc(gi, 4) if gi == 0 else stc(gi, 6)
-    rc = T.st[:, 56:58]
-    blk = lambda buf, gi, b, w: buf[:, (gi * 2 + b) * w:(gi * 2 + b + 1) * w]
-    Exp = ActivationFunctionType.Exp
+    ncol, nun, seen = [0], [0], []
 
+    def col(n):
+        ncol[0] += n
+        return T.st[:, ncol[0] - n:ncol[0]]
+    blk = lambda buf, gi, b, w: buf[:, (gi * 2 + b) * w:(gi * 2 + b + 1) * w]
+    pcols = lambda buf, u: buf[:, (u[0] * 4 + u[2][0]) * 256:(u[0] * 4 + u[2][-1] + 1) * 256]
+    sap = lambda u: SB[u[0]][u[1]][:, (u[2][0] % 2) * 256:(u[2][-1] % 2 + 1) * 256]
+    Exp, MIN = ActivationFunctionType.Exp, AluOpType.min
     order = [mykind] + [k for k in DUE if k != mykind]
-    te.wait_ge(eidn, 1)
-    eo_prev, l_ready = None, None
-    for gi, kd in enumerate(order):
-        if gi == 0:
-            buf, c0 = T.own, D
+
+    def kvof(j):
+        return (T.own, D) if j == 0 else (T.kv, hosts.index(nb[C][order[j]]) * 512)
+
+    def arrive(j):
+        if j in seen:
+            return
+        seen.append(j)
+        if j == 0:
             for s, v in own_waits:
                 te.wait_ge(s, v)
         else:
-            sl = hosts.index(nb[C][kd])
-            buf, c0 = T.kv, sl * 512
-            te.wait_ge(sem["kv%d" % sl], cnt(m_up) if kd == "own" else cnt(m_on))
-        kk = buf[:, c0 + D:c0 + 3 * D]
-        vv = [buf[:, c0:c0 + D], buf[:, c0 + 3 * D:c0 + 4 * D]]
-        Sg = [S[gi % 2][b][:, 0:256] for b in (0, 1)]
-        es, ered, ep, et, ec, eo = [ev(), ev()], ev(), [ev(), ev()], [ev(), ev()], [ev(), ev()], [ev(), ev()]
-        for b in (0, 1):
-            te.matmul(Sg[b], q[b], kk, True, True).then_inc(es[b], 1)
-        for b in (0, 1):
-            ve.wait_ge(es[b], 1)
-            ve.tensor_reduce(nmg(gi)[:, b:b + 1], Sg[b], AxisListType.X, AluOpType.max, negate=True).then_inc(ered, 1)
-        ve.wait_ge(ered, 2)
+            te.wait_ge(sem["kv%d" % hosts.index(nb[C][order[j]])], cnt(m_up) if order[j] == "own" else cnt(m_on))
+
+    plan = [[0, 1, 2, 3]] if idx == 1 else [[0], [1], [2], [3]]
+    te.wait_ge(eidn, 1)
+    eo_prev, l_ready, nm_prev, l_prev = None, [], None, None
+    for gi, subs in enumerate(plan):
+        hs = sorted({j // 2 for j in subs})
+        nh = len(hs)
+        units = [(b, h, [j for j in subs if j // 2 == h]) for b in (0, 1) for h in hs]
+        nu = len(units)
+        es, ep, et, ec = [[ev() for _ in units] for _ in range(4)]
+        eo, ered = [ev(), ev()], [ev(), ev()]
+        pbank = [PT[(nun[0] + ui) % 2] for ui in range(nu)]
+        nun[0] += nu
+        for ui, u in enumerate(units):
+            for j in u[2]:
+                arrive(j)
+                buf, c0 = kvof(j)
+                te.matmul(SB[u[0]][u[1]][:, (j % 2) * 256:(j % 2 + 1) * 256], q[u[0]], buf[:, c0 + D:c0 + 3 * D],
+                          True, True).then_inc(es[ui], 1)
+        nmg = col(2 * nh)
+        nmn = nmg if (nh == 1 and gi == 0) else col(2)
+        nmr = [None, None]
+        for ui, u in enumerate(units):
+            b, i = u[0], hs.index(u[1])
+            ve.wait_ge(es[ui], len(u[2]))
+            ve.tensor_reduce(nmg[:, b * nh + i:b * nh + i + 1], sap(u), AxisListType.X, AluOpType.max,
+                             negate=True).then_inc(ered[b], 1)
+            if nh == 2 and i == 1:
+                e = ev()
+                ve.wait_ge(ered[b], 2)
+                ve.tensor_tensor(nmn[:, b:b + 1], nmg[:, 2 * b:2 * b + 1], nmg[:, 2 * b + 1:2 * b + 2], MIN).then_inc(e, 1)
+                nmr[b] = (e, 1)
+        if nh == 1:
+            ve.wait_ge(ered[0], 1)
+            ve.wait_ge(ered[1], 1)
+            nmr = [(ered[0], 1), (ered[1], 1)]
         if gi > 0:
             enm, ed, eal, ers = ev(), ev(), ev(), [ev(), ev()]
-            ve.tensor_tensor(nm(gi), nm(gi - 1), nmg(gi), AluOpType.min).then_inc(enm, 1)
+            dd, al = col(2), col(2)
+            ve.tensor_tensor(nmn, nm_prev, nmg, MIN).then_inc(enm, 1)
             ve.wait_ge(enm, 1)
-            ve.tensor_tensor(dd(gi), nm(gi), nm(gi - 1), AluOpType.subtract).then_inc(ed, 1)
-            ac.wait_ge(enm, 1)
-        else:
-            ac.wait_ge(ered, 2)
-        ac.activation(blk(T.p, gi, 0, 256), Sg[0], Exp, bias=nm(gi)[:, 0:1], scale=1.0,
-                      accum_out=lg(gi)[:, 0:1]).then_inc(ep[0], 1)
-        if gi > 0:
-            ac.wait_ge(ed, 1)
-            ac.activation(al(gi), dd(gi), Exp).then_inc(eal, 1)
-        ac.activation(blk(T.p, gi, 1, 256), Sg[1], Exp, bias=nm(gi)[:, 1:2], scale=1.0,
-                      accum_out=lg(gi)[:, 1:2]).then_inc(ep[1], 1)
+            ve.tensor_tensor(dd, nmn, nm_prev, AluOpType.subtract).then_inc(ed, 1)
+            nmr = [(enm, 1), (enm, 1)]
+        lgc = col(2 * nh)
+        for ui, u in enumerate(units):
+            b, i = u[0], hs.index(u[1])
+            ac.wait_ge(nmr[b][0], nmr[b][1])
+            ac.activation(pcols(T.p, u), sap(u), Exp, bias=nmn[:, b:b + 1], scale=1.0,
+                          accum_out=lgc[:, i * 2 + b:i * 2 + b + 1]).then_inc(ep[ui], 1)
+            if gi > 0 and ui == 0:
+                ac.wait_ge(ed, 1)
+                ac.activation(al, dd, Exp).then_inc(eal, 1)
         if gi > 0:
             ve.wait_ge(eal, 1)
             for b in (0, 1):
                 ve.wait_ge(eo_prev[b][0], eo_prev[b][1])
-                ve.tensor_scalar(blk(T.oo, gi, b, D), O[b][:, 0:D], al(gi)[:, b:b + 1], None,
+                ve.tensor_scalar(blk(T.oo, gi, b, D), O[b][:, 0:D], al[:, b:b + 1], None,
                                  AluOpType.mult).then_inc(ers[b], 1)
-        for b in (0, 1):
-            te.wait_ge(ep[b], 1)
-            for j in (0, 1):
-                te.transpose(PT[b][:, j * D:(j + 1) * D], blk(T.p, gi, b, 256)[:, j * D:(j + 1) * D],
-                             T.idn[:]).then_inc(et[b], 1)
-            if gi > 0:
-                te.wait_ge(ers[b], 1)
-                te.matmul(O[b][:, 0:D], T.idn[:], blk(T.oo, gi, b, D), True, False).then_inc(eo[b], 1)
-        for b in (0, 1):
-            ve.wait_ge(et[b], 2)
-            ve.tensor_copy(blk(T.pts, gi, b, 256), PT[b][:, 0:256]).then_inc(ec[b], 1)
-        for b in (0, 1):
-            te.wait_ge(ec[b], 1)
-            te.matmul(O[b][:, 0:D], blk(T.pts, gi, b, 256)[:, 0:D], vv[0], gi == 0, False).then_inc(eo[b], 1)
-            te.matmul(O[b][:, 0:D], blk(T.pts, gi, b, 256)[:, D:2 * D], vv[1], False, True).then_inc(eo[b], 1)
-        eo_prev = [(eo[b], 2 if gi == 0 else 3) for b in (0, 1)]
+        nmm = [sum(2 * len(u[2]) for u in units if u[0] == b) + (1 if gi > 0 else 0) for b in (0, 1)]
+        done = [0, 0]
+        for step in range(nu + 1):
+            if step < nu:
+                u = units[step]
+                te.wait_ge(ep[step], 1)
+                for t in range(2 * len(u[2])):
+                    te.transpose(pbank[step][:, t * D:(t + 1) * D], pcols(T.p, u)[:, t * D:(t + 1) * D],
+                                 T.idn[:]).then_inc(et[step], 1)
+                if gi > 0 and done[u[0]] == 0:
+                    te.wait_ge(ers[u[0]], 1)
+                    te.matmul(O[u[0]][:, 0:D], T.idn[:], blk(T.oo, gi, u[0], D), True, False).then_inc(eo[u[0]], 1)
+                    done[u[0]] += 1
+            if step > 0:
+                u = units[step - 1]
+                te.wait_ge(ec[step - 1], 1)
+                for t in range(2 * len(u[2])):
+                    buf, c0 = kvof(u[2][t // 2])
+                    c0 += 0 if t % 2 == 0 else 3 * D
+                    done[u[0]] += 1
+                    te.matmul(O[u[0]][:, 0:D], pcols(T.pts, u)[:, t * D:(t + 1) * D], buf[:, c0:c0 + D],
+                              done[u[0]] == 1, done[u[0]] == nmm[u[0]]).then_inc(eo[u[0]], 1)
+        for ui, u in enumerate(units):
+            ve.wait_ge(et[ui], 2 * len(u[2]))
+            ve.tensor_copy(pcols(T.pts, u), pbank[ui][:, 0:256 * len(u[2])]).then_inc(ec[ui], 1)
+        eo_prev = [(eo[b], nmm[b]) for b in (0, 1)]
+        for e in ep:
+            ve.wait_ge(e, 1)
+        lsum = lgc
+        if nh == 2:
+            lsum, e = col(2), ev()
+            ve.tensor_tensor(lsum, lgc[:, 0:2], lgc[:, 2:4], AluOpType.add).then_inc(e, 1)
+            l_ready = l_ready + [(e, 1)]
         if gi > 0:
-            etmp, el = ev(), ev()
+            etmp, el, tmp, lnew = ev(), ev(), col(2), col(2)
             for s, v in l_ready:
                 ve.wait_ge(s, v)
-            ve.tensor_tensor(tmp(gi), ll(gi - 1), al(gi), AluOpType.mult).then_inc(etmp, 1)
+            ve.tensor_tensor(tmp, l_prev, al, AluOpType.mult).then_inc(etmp, 1)
             ve.wait_ge(etmp, 1)
-            ve.wait_ge(ep[0], 1)
-            ve.wait_ge(ep[1], 1)
-            ve.tensor_tensor(ll(gi), tmp(gi), lg(gi), AluOpType.add).then_inc(el, 1)
-            l_ready = [(el, 1)]
-        else:
-            l_ready = [(ep[0], 1), (ep[1], 1)]
+            ve.tensor_tensor(lnew, tmp, lsum, AluOpType.add).then_inc(el, 1)
+            lsum, l_ready = lnew, [(el, 1)]
+        nm_prev, l_prev = nmn, lsum
+    rc = col(2)
     er, ey = ev(), [ev(), ev()]
     for s, v in l_ready:
         ve.wait_ge(s, v)
-    ve.reciprocal(rc, ll(len(order) - 1)).then_inc(er, 1)
+    ve.reciprocal(rc, l_prev).then_inc(er, 1)
     ve.wait_ge(er, 1)
     ve.wait_ge(eo_prev[0][0], eo_prev[0][1])
     ve.tensor_scalar(T.yo[:, 0:D], O[0][:, 0:D], rc[:, 0:1], None, AluOpType.mult).then_inc(ey[0], 1)
@@ -275,13 +337,7 @@ def rank_program(g, core, T, topo):
         for kd, val in (("own", cnt(m_up)), ("cb", 2 * cnt(half[0])), ("sw", 2 * cnt(half[0])), ("dg", 2 * cnt(m_off))):
             hs = sorted(h for h in ranks_of[nb[C][kd]] if h != head)
             sy.wait_ge(sem["ya%d" % hosts.index(nb[C][kd])], val)
-            runs = [[hs[0], hs[0]]]
-            for h in hs[1:]:
-                if h == runs[-1][1] + 1:
-                    runs[-1][1] = h
-                else:
-                    runs.append([h, h])
-            for lo, hi in runs:
+            for lo, hi in _runs(hs):
                 sy.dma_start(T.y[:, lo * D:(hi + 1) * D], T.yl[:, lo * D:(hi + 1) * D]).then_inc(sem.st, 16)
                 nst += 1
         sy.wait_ge(sem.st, 16 * nst)

@@ -27,7 +27,7 @@ SEMAPHORES = (["ld", "ld2", "st", "snt", "own", "rl", "rl2", "rpd", "rpx", "rpo"
               + ["kv%d" % i for i in range(4)] + ["ya%d" % i for i in range(4)] + ["e%d" % i for i in range(NEV)])
 
 IDX = {"own": 0, "dg": 1, "sw": 2, "cb": 3}
-DUE = ["own", "dg", "cb", "sw"]
+DUE = ["own", "cb", "sw", "dg"]
 
 
 def _bits(m):
@@ -91,6 +91,7 @@ def rank_program(g, core, T, topo):
 
     te, ve, ac, sy, sem = g.tensor, g.vector, g.scalar, g.sync, T.sem
     nev, sent = [0], [0]
+    Exp, MIN = ActivationFunctionType.Exp, AluOpType.min
 
     def ev():
         nev[0] += 1
@@ -111,7 +112,13 @@ def rank_program(g, core, T, topo):
         g.remote_dma_fused(trs, local_sem=sem.snt)
 
     eone, eidn = ev(), ev()
-    ve.memset(T.ones[:], 1.0).then_inc(eone, 1)
+    if idx == 0:
+        ve.memset(T.ones[:], 1.0).then_inc(eone, 1)
+    else:
+        ezero = ev()
+        ve.memset(T.ones[:], 0.0).then_inc(ezero, 1)
+        ac.wait_ge(ezero, 1)
+        ac.activation(T.ones[:], T.ones[:], Exp).then_inc(eone, 1)
     g.wait_ge(eone, 1)
     g.affine_select(T.idn[:], T.ones[:], [[-1, D]], AluOpType.is_equal, 0.0, 0, 1).then_inc(eidn, 1)
 
@@ -183,7 +190,6 @@ def rank_program(g, core, T, topo):
     blk = lambda buf, gi, b, w: buf[:, (gi * 2 + b) * w:(gi * 2 + b + 1) * w]
     pcols = lambda buf, u: buf[:, (u[0] * 4 + u[2][0]) * 256:(u[0] * 4 + u[2][-1] + 1) * 256]
     sap = lambda u: SB[u[0]][u[1]][:, (u[2][0] % 2) * 256:(u[2][-1] % 2 + 1) * 256]
-    Exp, MIN = ActivationFunctionType.Exp, AluOpType.min
     order = [mykind] + [k for k in DUE if k != mykind]
 
     def kvof(j):
@@ -310,22 +316,25 @@ def rank_program(g, core, T, topo):
     ac.wait_ge(eo_prev[1][0], eo_prev[1][1])
     ac.activation(T.yo[:, D:2 * D], O[1][:, 0:D], ActivationFunctionType.Identity, scale=rc[:, 1:2]).then_inc(ey[1], 1)
 
-    g.wait_ge(ey[0], 1)
-    g.wait_ge(ey[1], 1)
     ycol = lambda h: T.yl[:, h * D:(h + 1) * D]
     yblk = lambda i: T.yo[:, i * D:(i + 1) * D]
     ya = sem["ya%d" % hosts.index(C)]
-    if idx == 0:
-        send([tr(yblk(1 - myb), ycol(head), [cores[other]], m_up, ya)])
-    elif idx == 1:
+    if idx == 1:
         relg = group[head_on(nb[C]["sw"], topo.die(core))]
-        send([tr(yblk(i), T.rl2[:], [relg[i]], half[i], sem.rl2) for i in (0, 1)])
+        for i in (0, 1):
+            g.wait_ge(ey[i], 1)
+            send([tr(yblk(i), T.rl2[:], [relg[i]], m_off, sem.rl2)])
     else:
-        send([tr(yblk(i), ycol(head), [cores[sr[i]]], half[i], ya) for i in (0, 1)])
+        g.wait_ge(ey[0], 1)
+        g.wait_ge(ey[1], 1)
+        if idx == 0:
+            send([tr(yblk(1 - myb), ycol(head), [cores[other]], m_up, ya)])
+        else:
+            send([tr(yblk(i), ycol(head), [cores[sr[i]]], half[i], ya) for i in (0, 1)])
     if idx <= 1:
         A = nb[C]["sw"]
         hh = head_on(A, topo.die(core))
-        g.wait_ge(sem.rl2, cnt(half[0]))
+        g.wait_ge(sem.rl2, cnt(m_off))
         send([tr(T.rl2[:], ycol(hh), [cores[ranks_of[nb[A]["dg"]][idx]]], m_off, sem["ya%d" % hosts.index(A)])])
     g.wait_ge(sem.snt, sent[0])
 

@@ -12,7 +12,6 @@ SCRATCH = {
     "x": ("sbuf", [128, 8 * PK], "bfloat16"),
     "own": ("sbuf", [128, 2 * PK], "bfloat16"),
     "kv": ("sbuf", [128, 4 * 512], "bfloat16"),
-    "rl": ("sbuf", [128, PK], "bfloat16"), "rl2": ("sbuf", [128, D], "bfloat16"),
     "p": ("sbuf", [128, 8 * 256], "bfloat16"), "pts": ("sbuf", [128, 8 * 256], "bfloat16"),
     "oo": ("sbuf", [128, 8 * D], "bfloat16"),
     "st": ("sbuf", [128, 64], "float32"),
@@ -23,11 +22,8 @@ SCRATCH = {
     "pt0": ("psum", [128, 1024], "bfloat16"), "pt1": ("psum", [128, 1024], "bfloat16"),
     "o0": ("psum", [128, 512], "float32"), "o1": ("psum", [128, 512], "float32"),
 }
-SEMAPHORES = (["ld", "ld2", "st", "snt", "own", "rl", "rl2", "rpd", "rpx", "rpo", "rpc", "rps"]
-              + ["kv%d" % i for i in range(4)] + ["ya%d" % i for i in range(4)] + ["e%d" % i for i in range(NEV)])
-
-IDX = {"own": 0, "dg": 1, "sw": 2, "cb": 3}
-DUE = ["own", "cb", "sw", "dg"]
+SEMAPHORES = (["ld", "ldq", "ld2", "st", "st2", "snt", "ow0", "ow1", "oq", "rpd", "rpe", "rpx", "rpo", "yx", "yy",
+               "ks", "kc0", "kc1", "kf0", "kf1"] + ["e%d" % i for i in range(NEV)])
 
 
 def _bits(m):
@@ -36,16 +32,6 @@ def _bits(m):
 
 def _mask(lst):
     return sum(1 << i for i in lst)
-
-
-def _runs(hs):
-    runs = [[hs[0], hs[0]]]
-    for h in hs[1:]:
-        if h == runs[-1][1] + 1:
-            runs[-1][1] = h
-        else:
-            runs.append([h, h])
-    return runs
 
 
 def rank_program(g, core, T, topo):
@@ -66,27 +52,35 @@ def rank_program(g, core, T, topo):
             return "dg"
         return "sw" if topo.same_plane(a, b) else "cb"
     nb = {A: {kind(A, B): B for B in hosts} for A in hosts}
-    group = {}
-    for h, c in enumerate(cores):
-        group[h] = [c] + sorted(x for x in range(NSIM) if x != c and topo.host(x) == topo.host(c)
-                                and topo.chip(x) == topo.chip(c) and topo.die(x) == topo.die(c))
+    cls = {H: (0 if H in (hosts[0], nb[hosts[0]]["cb"]) else 1) for H in hosts}
+    nhc = len(cores) // 2
+    HC = [list(range(nhc)), list(range(nhc, 2 * nhc))]
+    dcs = {}
+    for c in cores:
+        dcs[c] = [c] + sorted(x for x in range(NSIM) if x != c and topo.host(x) == topo.host(c)
+                              and topo.chip(x) == topo.chip(c) and topo.die(x) == topo.die(c))
 
-    def head_on(H, die):
-        return [h for h in ranks_of[H] if topo.die(cores[h]) == die][0]
+    def server(H, h, role):
+        i = HC[cls[H]].index(h)
+        return dcs[cores[ranks_of[H][i // 2]]][2 * role + i % 2]
 
-    head = [h for h in group if core in group[h]][0]
-    idx = group[head].index(core)
     C = topo.host(core)
-    mykind = [k for k in IDX if IDX[k] == idx][0]
-    src_host = nb[C][mykind]
+    myb = [d for d, r in enumerate(ranks_of[C]) if core in dcs[cores[r]]][0]
+    pos = dcs[cores[ranks_of[C][myb]]].index(core)
+    role, is_rank = pos // 2, pos == 0
+    head = HC[cls[C]][2 * myb + pos % 2]
+    src_host = C if role == 0 else nb[C]["sw"]
     sr = ranks_of[src_host]
-    sibs = [x for x in group[head] if x != core]
+    sib = server(C, head, 1 - role)
+    far = server(nb[C]["cb"], head, role)
 
-    m_on = topo.mask(core, sibs[0])
-    m_off = topo.mask(core, cores[ranks_of[nb[C]["sw"]][0]])
+    m_on = topo.mask(core, sib)
+    m_off = topo.mask(core, far)
     offb = _bits(m_off)
     half = [_mask(offb[:len(offb) // 2]), _mask(offb[len(offb) // 2:])]
+    quar = [_mask(offb[i * len(offb) // 4:(i + 1) * len(offb) // 4]) for i in range(4)]
     m_up = m_on & ~m_off
+    upb = _bits(m_up)
     cnt = lambda m: len(_bits(m))
 
     te, ve, ac, sy, sem = g.tensor, g.vector, g.scalar, g.sync, T.sem
@@ -97,22 +91,17 @@ def rank_program(g, core, T, topo):
         nev[0] += 1
         return sem["e%d" % (nev[0] - 1)]
 
-    def tr(src, dst, dests, mask, rsem):
-        ids = []
-        for d in dests:
-            rid, pid = topo.addr(d, core)
-            ids.append(DstId(rid=rid, pnc=pid))
+    def tr(src, dst, dest, mask, rsem):
+        rid, pid = topo.addr(dest, core)
         sent[0] += cnt(mask)
-        if len(dests) == 1:
-            return RemoteDMATransfer(dst_ids=ids, dma_engine_mask=mask, remote_sem=rsem, src=src, dst=dst)
-        return RemoteDMATransfer(dst_ids=ids, dma_engine_mask=mask, remote_sem=rsem, srcs=[src],
-                                 dsts=[dst for _ in dests])
+        return RemoteDMATransfer(dst_ids=[DstId(rid=rid, pnc=pid)], dma_engine_mask=mask, remote_sem=rsem,
+                                 src=src, dst=dst)
 
     def send(trs):
         g.remote_dma_fused(trs, local_sem=sem.snt)
 
     eone, eidn = ev(), ev()
-    if idx == 0:
+    if is_rank:
         ve.memset(T.ones[:], 1.0).then_inc(eone, 1)
     else:
         ezero = ev()
@@ -122,62 +111,75 @@ def rank_program(g, core, T, topo):
     g.wait_ge(eone, 1)
     g.affine_select(T.idn[:], T.ones[:], [[-1, D]], AluOpType.is_equal, 0.0, 0, 1).then_inc(eidn, 1)
 
-    own_waits = [(sem.own, {0: cnt(m_up), 1: 2 * cnt(m_off), 2: 2 * cnt(half[0]), 3: 2 * cnt(half[0])}[idx])]
-    myb, other = 0, 0
-    if idx == 0:
-        myb = ranks_of[C].index(head)
-        other = [h for h in ranks_of[C] if h != head][0]
-        parts = [sorted(ranks_of[nb[C]["dg"]] + ranks_of[nb[C]["cb"]]), sorted(ranks_of[C] + ranks_of[nb[C]["sw"]])]
-        nld = [0, 0]
-        for pi, (hs, s) in enumerate(zip(parts, (sem.ld, sem.ld2))):
-            for lo, hi in _runs(hs):
-                for ti, (buf, t) in enumerate(((T.ql, T.q), (T.kl, T.k), (T.vl, T.v))):
-                    qu = sy if (ti + pi) % 2 == 0 else ac
-                    qu.dma_start(buf[:, lo * D:(hi + 1) * D], t[:, lo * D:(hi + 1) * D]).then_inc(s, 16)
-                    nld[pi] += 16
-        ve.wait_ge(sem.ld, nld[0])
+    m_big, m_sm = _mask(upb[:len(upb) // 2]), [_mask(upb[len(upb) // 2:3 * len(upb) // 4]), _mask(upb[3 * len(upb) // 4:])]
+    if role == 1:
+        pc_waits = [(sem.ow0, cnt(half[0])), (sem.ow1, cnt(half[0]))]
+        own_waits = pc_waits + [(sem.oq, 2 * cnt(quar[0]))]
+    elif is_rank:
+        pc_waits = own_waits = [(sem.rpo, 3), (sem.ow1, cnt(m_big))]
+    else:
+        pc_waits = own_waits = [(sem.ow0, cnt(m_sm[0])), (sem.ow1, cnt(m_sm[0]))]
+    Xh, Yh = HC[cls[C]], HC[1 - cls[C]]
+    xlo, xhi, ylo, yhi = Xh[0] * D, (Xh[-1] + 1) * D, Yh[0] * D, (Yh[-1] + 1) * D
+    if is_rank:
+        other = cores[ranks_of[C][1 - myb]]
+        sy.dma_start(T.vl[:, ylo:yhi], T.v[:, ylo:yhi]).then_inc(sem.ld, 16)
+        ac.dma_start(T.kl[:, ylo:yhi], T.k[:, ylo:yhi]).then_inc(sem.ld, 16)
+        sy.dma_start(T.ql[:, ylo:yhi], T.q[:, ylo:yhi]).then_inc(sem.ldq, 16)
+        ac.dma_start(T.vl[:, xlo:xhi], T.v[:, xlo:xhi]).then_inc(sem.ld2, 16)
+        sy.dma_start(T.kl[:, xlo:xhi], T.k[:, xlo:xhi]).then_inc(sem.ld2, 16)
+        ac.dma_start(T.ql[:, xlo:xhi], T.q[:, xlo:xhi]).then_inc(sem.ld2, 16)
         oq, ok = (0, 2 * D) if myb == 0 else (2 * D, 0)
+        okv = min(D, ok)
 
-        def pack(h, out, o0, s):
-            for buf, off in ((T.ql, oq), (T.vl, D), (T.kl, ok)):
+        def pack(h, out, o0, s, bufs):
+            for buf, off in bufs:
                 ve.tensor_copy(out[:, o0 + off:o0 + off + D], buf[:, h * D:(h + 1) * D]).then_inc(s, 1)
-        for h in ranks_of[nb[C]["dg"]]:
-            pack(h, T.x, h * PK, sem.rpd)
-        for h in ranks_of[nb[C]["cb"]]:
-            pack(h, T.x, h * PK, sem.rpc)
-        ve.wait_ge(sem.ld2, nld[1])
-        pack(other, T.x, other * PK, sem.rpx)
-        pack(head, T.own, myb * PK, sem.rpo)
-        for h in ranks_of[nb[C]["sw"]]:
-            pack(h, T.x, h * PK, sem.rps)
-        own_waits.append((sem.rpo, 3))
+        ve.wait_ge(sem.ld, 32)
+        nyh = len(Yh) // 2
+        Y1, Y2 = Yh[myb * nyh:(myb + 1) * nyh], Yh[(1 - myb) * nyh:(2 - myb) * nyh]
+        for hs_, s_ in ((Y1, sem.rpd), (Y2, sem.rpe)):
+            for h in hs_:
+                pack(h, T.x, h * PK, s_, ((T.vl, D), (T.kl, ok)))
+        ve.wait_ge(sem.ld2, 48)
+        full = ((T.ql, oq), (T.vl, D), (T.kl, ok))
+        for h in Xh:
+            if h != head:
+                pack(h, T.x, h * PK, sem.rpx, full)
+        pack(head, T.own, myb * PK, sem.rpo, full)
 
-        land = T.own[:, myb * PK:(myb + 1) * PK]
-        pk = lambda h: T.x[:, h * PK:(h + 1) * PK]
-        relg = group[head_on(nb[C]["sw"], topo.die(core))]
-        g.wait_ge(sem.rpd, 6)
-        send([tr(pk(h), T.rl[:], [relg[2 + i]], half[i], sem.rl) for i, h in enumerate(ranks_of[nb[C]["dg"]])])
-        for kd, s in (("cb", sem.rpc), ("own", sem.rpx), ("sw", sem.rps)):
-            if kd == "own":
-                g.wait_ge(s, 3)
-                send([tr(pk(other), land, [cores[other]], m_up, sem.own)])
-                continue
-            g.wait_ge(s, 6)
-            send([tr(pk(h), land, [group[h][IDX[kind(nb[C][kd], C)]]], half[i], sem.own)
-                  for i, h in enumerate(ranks_of[nb[C][kd]])])
-    elif idx >= 2:
-        A = nb[C]["sw"]
-        rr = head_on(A, topo.die(core))
-        hh = ranks_of[nb[A]["dg"]][idx - 2]
-        bb = ranks_of[A].index(rr)
-        g.wait_ge(sem.rl, cnt(half[0]))
-        send([tr(T.rl[:], T.own[:, bb * PK:(bb + 1) * PK], [group[hh][IDX["dg"]]], m_off, sem.own)])
+        B = nb[C]["sw"]
+        for hs_, s_, d_ in ((Y1, sem.rpd, sem.ow0), (Y2, sem.rpe, sem.ow1)):
+            g.wait_ge(s_, 2 * len(hs_))
+            send([tr(T.x[:, h * PK + okv:h * PK + okv + 2 * D], T.own[:, myb * PK + okv:myb * PK + okv + 2 * D],
+                     server(B, h, 1), half[i], d_) for i, h in enumerate(hs_)])
+        g.wait_ge(sem.ldq, 16)
+        send([tr(T.ql[:, h * D:(h + 1) * D], T.own[:, myb * PK + oq:myb * PK + oq + D],
+                 server(B, h, 1), quar[i], sem.oq) for i, h in enumerate(Yh)])
+        g.wait_ge(sem.rpx, 3 * (len(Xh) - 1))
+        trs, sm = [], list(m_sm)
+        for h in Xh:
+            if h != head:
+                a = server(C, h, 0)
+                trs.append(tr(T.x[:, h * PK:(h + 1) * PK], T.own[:, myb * PK:(myb + 1) * PK], a,
+                              m_big if a == other else sm.pop(0), sem.ow0 if a in dcs[core] else sem.ow1))
+        send(trs)
 
-    m_fw = m_up if idx == 0 else m_on
-    for s, v in own_waits:
-        g.wait_ge(s, v)
     slot = hosts.index(src_host)
-    send([tr(T.own[:, D:D + 512], T.kv[:, slot * 512:(slot + 1) * 512], sibs, m_fw, sem["kv%d" % slot])])
+    pcs = (myb, 1 - myb)
+    for n, p in enumerate(pcs):
+        g.wait_ge(pc_waits[n][0], pc_waits[n][1])
+        send([tr(T.own[:, D + p * 256:D + (p + 1) * 256], T.kv[:, slot * 512 + p * 256:slot * 512 + (p + 1) * 256],
+                 far, m_off, sem["kc%d" % n])])
+    send([tr(T.own[:, D:D + 512], T.kv[:, slot * 512:(slot + 1) * 512], sib, m_up, sem.ks)])
+    order = ["own", "sw", "cb", "dg"] if role == 0 else ["sw", "own", "dg", "cb"]
+    due = [own_waits, [(sem.ks, cnt(m_up))], [(sem.kc0, cnt(m_off)), (sem.kc1, cnt(m_off))],
+           [(sem.kf0, cnt(m_on)), (sem.kf1, cnt(m_on))]]
+    cslot = hosts.index(nb[C][order[2]])
+    for n, p in enumerate(pcs):
+        g.wait_ge(due[2][n][0], due[2][n][1])
+        send([tr(T.kv[:, cslot * 512 + p * 256:cslot * 512 + (p + 1) * 256],
+                 T.kv[:, cslot * 512 + p * 256:cslot * 512 + (p + 1) * 256], sib, m_on, sem["kf%d" % n])])
 
     SB = [[T.s00, T.s10], [T.s01, T.s11]]
     PT, O = [T.pt0, T.pt1], [T.o0, T.o1]
@@ -190,7 +192,6 @@ def rank_program(g, core, T, topo):
     blk = lambda buf, gi, b, w: buf[:, (gi * 2 + b) * w:(gi * 2 + b + 1) * w]
     pcols = lambda buf, u: buf[:, (u[0] * 4 + u[2][0]) * 256:(u[0] * 4 + u[2][-1] + 1) * 256]
     sap = lambda u: SB[u[0]][u[1]][:, (u[2][0] % 2) * 256:(u[2][-1] % 2 + 1) * 256]
-    order = [mykind] + [k for k in DUE if k != mykind]
 
     def kvof(j):
         return (T.own, D) if j == 0 else (T.kv, hosts.index(nb[C][order[j]]) * 512)
@@ -199,13 +200,10 @@ def rank_program(g, core, T, topo):
         if j in seen:
             return
         seen.append(j)
-        if j == 0:
-            for s, v in own_waits:
-                te.wait_ge(s, v)
-        else:
-            te.wait_ge(sem["kv%d" % hosts.index(nb[C][order[j]])], cnt(m_up) if order[j] == "own" else cnt(m_on))
+        for s, v in due[j]:
+            te.wait_ge(s, v)
 
-    plan = [[0, 1, 2, 3]] if idx == 1 else [[0], [1], [2], [3]]
+    plan = [[0], [1], [2], [3]]
     te.wait_ge(eidn, 1)
     eo_prev, l_ready, nm_prev, l_prev = None, [], None, None
     for gi, subs in enumerate(plan):
@@ -231,15 +229,9 @@ def rank_program(g, core, T, topo):
             ve.wait_ge(es[ui], len(u[2]))
             ve.tensor_reduce(nmg[:, b * nh + i:b * nh + i + 1], sap(u), AxisListType.X, AluOpType.max,
                              negate=True).then_inc(ered[b], 1)
-            if nh == 2 and i == 1:
-                e = ev()
-                ve.wait_ge(ered[b], 2)
-                ve.tensor_tensor(nmn[:, b:b + 1], nmg[:, 2 * b:2 * b + 1], nmg[:, 2 * b + 1:2 * b + 2], MIN).then_inc(e, 1)
-                nmr[b] = (e, 1)
-        if nh == 1:
-            ve.wait_ge(ered[0], 1)
-            ve.wait_ge(ered[1], 1)
-            nmr = [(ered[0], 1), (ered[1], 1)]
+        ve.wait_ge(ered[0], 1)
+        ve.wait_ge(ered[1], 1)
+        nmr = [(ered[0], 1), (ered[1], 1)]
         if gi > 0:
             enm, ed, eal, ers = ev(), ev(), ev(), [ev(), ev()]
             dd, al = col(2), col(2)
@@ -291,10 +283,6 @@ def rank_program(g, core, T, topo):
         for e in ep:
             ve.wait_ge(e, 1)
         lsum = lgc
-        if nh == 2:
-            lsum, e = col(2), ev()
-            ve.tensor_tensor(lsum, lgc[:, 0:2], lgc[:, 2:4], AluOpType.add).then_inc(e, 1)
-            l_ready = l_ready + [(e, 1)]
         if gi > 0:
             etmp, el, tmp, lnew = ev(), ev(), col(2), col(2)
             for s, v in l_ready:
@@ -304,6 +292,10 @@ def rank_program(g, core, T, topo):
             ve.tensor_tensor(lnew, tmp, lsum, AluOpType.add).then_inc(el, 1)
             lsum, l_ready = lnew, [(el, 1)]
         nm_prev, l_prev = nmn, lsum
+    ycol = lambda h: T.yl[:, h * D:(h + 1) * D]
+    outs = [T.yo[:, 0:D], T.yo[:, D:2 * D]]
+    if is_rank:
+        outs[myb] = ycol(head)
     rc = col(2)
     er, ey = ev(), [ev(), ev()]
     for s, v in l_ready:
@@ -311,42 +303,26 @@ def rank_program(g, core, T, topo):
     ve.reciprocal(rc, l_prev).then_inc(er, 1)
     ve.wait_ge(er, 1)
     ve.wait_ge(eo_prev[0][0], eo_prev[0][1])
-    ve.tensor_scalar(T.yo[:, 0:D], O[0][:, 0:D], rc[:, 0:1], None, AluOpType.mult).then_inc(ey[0], 1)
+    ve.tensor_scalar(outs[0], O[0][:, 0:D], rc[:, 0:1], None, AluOpType.mult).then_inc(ey[0], 1)
     ac.wait_ge(er, 1)
     ac.wait_ge(eo_prev[1][0], eo_prev[1][1])
-    ac.activation(T.yo[:, D:2 * D], O[1][:, 0:D], ActivationFunctionType.Identity, scale=rc[:, 1:2]).then_inc(ey[1], 1)
+    ac.activation(outs[1], O[1][:, 0:D], ActivationFunctionType.Identity, scale=rc[:, 1:2]).then_inc(ey[1], 1)
 
-    ycol = lambda h: T.yl[:, h * D:(h + 1) * D]
-    yblk = lambda i: T.yo[:, i * D:(i + 1) * D]
-    ya = sem["ya%d" % hosts.index(C)]
-    if idx == 1:
-        relg = group[head_on(nb[C]["sw"], topo.die(core))]
-        for i in (0, 1):
-            g.wait_ge(ey[i], 1)
-            send([tr(yblk(i), T.rl2[:], [relg[i]], m_off, sem.rl2)])
+    g.wait_ge(ey[0], 1)
+    g.wait_ge(ey[1], 1)
+    if is_rank:
+        send([tr(outs[1 - myb], ycol(head), cores[sr[1 - myb]], m_on, sem.yx)])
+    elif role == 0:
+        send([tr(outs[i], ycol(head), cores[sr[i]], (m_off, m_up)[i], sem.yx) for i in (0, 1)])
     else:
-        g.wait_ge(ey[0], 1)
-        g.wait_ge(ey[1], 1)
-        if idx == 0:
-            send([tr(yblk(1 - myb), ycol(head), [cores[other]], m_up, ya)])
-        else:
-            send([tr(yblk(i), ycol(head), [cores[sr[i]]], half[i], ya) for i in (0, 1)])
-    if idx <= 1:
-        A = nb[C]["sw"]
-        hh = head_on(A, topo.die(core))
-        g.wait_ge(sem.rl2, cnt(m_off))
-        send([tr(T.rl2[:], ycol(hh), [cores[ranks_of[nb[A]["dg"]][idx]]], m_off, sem["ya%d" % hosts.index(A)])])
+        send([tr(outs[i], ycol(head), cores[sr[i]], half[i], sem.yy) for i in (0, 1)])
     g.wait_ge(sem.snt, sent[0])
 
-    if idx == 0:
-        nst = 1
-        sy.wait_ge(ey[0], 1)
-        sy.wait_ge(ey[1], 1)
-        sy.dma_start(T.y[:, head * D:(head + 1) * D], yblk(myb)).then_inc(sem.st, 16)
-        for kd, val in (("own", cnt(m_up)), ("cb", 2 * cnt(half[0])), ("sw", 2 * cnt(half[0])), ("dg", 2 * cnt(m_off))):
-            hs = sorted(h for h in ranks_of[nb[C][kd]] if h != head)
-            sy.wait_ge(sem["ya%d" % hosts.index(nb[C][kd])], val)
-            for lo, hi in _runs(hs):
-                sy.dma_start(T.y[:, lo * D:(hi + 1) * D], T.yl[:, lo * D:(hi + 1) * D]).then_inc(sem.st, 16)
-                nst += 1
-        sy.wait_ge(sem.st, 16 * nst)
+    if is_rank:
+        sy.wait_ge(ey[myb], 1)
+        sy.wait_ge(sem.yx, cnt(m_on) + 2 * cnt(m_up))
+        sy.dma_start(T.y[:, xlo:xhi], T.yl[:, xlo:xhi]).then_inc(sem.st, 16)
+        ac.wait_ge(sem.yy, len(Yh) * cnt(half[0]))
+        ac.dma_start(T.y[:, ylo:yhi], T.yl[:, ylo:yhi]).then_inc(sem.st2, 16)
+        sy.wait_ge(sem.st, 16)
+        ac.wait_ge(sem.st2, 16)

@@ -184,7 +184,7 @@ def rank_program(g, core, T, topo):
     SB = [[T.s00, T.s10], [T.s01, T.s11]]
     PT, O = [T.pt0, T.pt1], [T.o0, T.o1]
     q = [T.own[:, 0:D], T.own[:, 5 * D:6 * D]]
-    ncol, nun, seen = [0], [0], []
+    ncol, nun = [0], [0]
 
     def col(n):
         ncol[0] += n
@@ -196,14 +196,7 @@ def rank_program(g, core, T, topo):
     def kvof(j):
         return (T.own, D) if j == 0 else (T.kv, hosts.index(nb[C][order[j]]) * 512)
 
-    def arrive(j):
-        if j in seen:
-            return
-        seen.append(j)
-        for s, v in due[j]:
-            te.wait_ge(s, v)
-
-    plan = [[0], [1], [2], [3]]
+    plan = [[0], [1], [2, 3]] if role == 0 else [[0, 1], [2, 3]]
     te.wait_ge(eidn, 1)
     eo_prev, l_ready, nm_prev, l_prev = None, [], None, None
     for gi, subs in enumerate(plan):
@@ -215,18 +208,27 @@ def rank_program(g, core, T, topo):
         eo, ered = [ev(), ev()], [ev(), ev()]
         pbank = [PT[(nun[0] + ui) % 2] for ui in range(nu)]
         nun[0] += nu
-        for ui, u in enumerate(units):
-            for j in u[2]:
-                arrive(j)
-                buf, c0 = kvof(j)
-                te.matmul(SB[u[0]][u[1]][:, (j % 2) * 256:(j % 2 + 1) * 256], q[u[0]], buf[:, c0 + D:c0 + 3 * D],
-                          True, True).then_inc(es[ui], 1)
+        nsc = [0] * nu
+        for j in subs:
+            buf, c0 = kvof(j)
+            if j >= 2:
+                parts = [([due[j][n]], pcs[n] * D, D) for n in (0, 1)]
+            else:
+                parts = [(due[j], 0, 2 * D)]
+            for waits, o, w in parts:
+                for s_, v_ in waits:
+                    te.wait_ge(s_, v_)
+                for ui, u in enumerate(units):
+                    if j in u[2]:
+                        te.matmul(SB[u[0]][u[1]][:, (j % 2) * 256 + o:(j % 2) * 256 + o + w], q[u[0]],
+                                  buf[:, c0 + D + o:c0 + D + o + w], True, True).then_inc(es[ui], 1)
+                        nsc[ui] += 1
         nmg = col(2 * nh)
         nmn = nmg if (nh == 1 and gi == 0) else col(2)
         nmr = [None, None]
         for ui, u in enumerate(units):
             b, i = u[0], hs.index(u[1])
-            ve.wait_ge(es[ui], len(u[2]))
+            ve.wait_ge(es[ui], nsc[ui])
             ve.tensor_reduce(nmg[:, b * nh + i:b * nh + i + 1], sap(u), AxisListType.X, AluOpType.max,
                              negate=True).then_inc(ered[b], 1)
         ve.wait_ge(ered[0], 1)

from concourse.bass import DstId, RemoteDMATransfer
from concourse.mybir import AluOpType, AxisListType, ActivationFunctionType

NSIM = 512
D = 128
PK = 3 * D
NEV = 84

SCRATCH = {
    "ql": ("sbuf", [128, 1024], "bfloat16"), "kl": ("sbuf", [128, 1024], "bfloat16"),
    "vl": ("sbuf", [128, 1024], "bfloat16"),
    "x": ("sbuf", [128, 8 * PK], "bfloat16"),
    "own": ("sbuf", [128, 2 * PK], "bfloat16"),
    "kv": ("sbuf", [128, 4 * 512], "bfloat16"),
    "p": ("sbuf", [128, 8 * 256], "bfloat16"), "pts": ("sbuf", [128, 8 * 256], "bfloat16"),
    "oo": ("sbuf", [128, 8 * D], "bfloat16"),
    "st": ("sbuf", [128, 64], "float32"),
    "yo": ("sbuf", [128, 2 * D], "bfloat16"), "yl": ("sbuf", [128, 1024], "bfloat16"),
    "ones": ("sbuf", [128, D], "bfloat16"), "idn": ("sbuf", [128, D], "bfloat16"),
    "s00": ("psum", [128, 512], "float32"), "s01": ("psum", [128, 512], "float32"),
    "s10": ("psum", [128, 512], "float32"), "s11": ("psum", [128, 512], "float32"),
    "pt0": ("psum", [128, 1024], "bfloat16"), "pt1": ("psum", [128, 1024], "bfloat16"),
    "o0": ("psum", [128, 512], "float32"), "o1": ("psum", [128, 512], "float32"),
}
SEMAPHORES = (["ld", "ldq", "ld2", "st", "st2", "snt", "ow0", "ow1", "oq", "rpd", "rpe", "rpx", "rpo", "yx", "yy",
               "ks", "kc0", "kc1", "kf0", "kf1"] + ["e%d" % i for i in range(NEV)])


def _bits(m):
    return [i for i in range(m.bit_length()) if (m >> i) & 1]


def _mask(lst):
    return sum(1 << i for i in lst)


def rank_program(g, core, T, topo):
    cores = [int(c) for c in T.cores]
    if not any(topo.host(c) == topo.host(core) and topo.chip(c) == topo.chip(core) for c in cores):
        return
    hosts = []
    for c in cores:
        if topo.host(c) not in hosts:
            hosts.append(topo.host(c))
    ranks_of = {H: [r for r, c in enumerate(cores) if topo.host(c) == H] for H in hosts}

    def kind(A, B):
        a, b = cores[ranks_of[A][0]], cores[ranks_of[B][0]]
        if A == B:
            return "own"
        if not topo.may_write(a, b):
            return "dg"
        return "sw" if topo.same_plane(a, b) else "cb"
    nb = {A: {kind(A, B): B for B in hosts} for A in hosts}
    cls = {H: (0 if H in (hosts[0], nb[hosts[0]]["cb"]) else 1) for H in hosts}
    nhc = len(cores) // 2
    HC = [list(range(nhc)), list(range(nhc, 2 * nhc))]
    dcs = {}
    for c in cores:
        dcs[c] = [c] + sorted(x for x in range(NSIM) if x != c and topo.host(x) == topo.host(c)
                              and topo.chip(x) == topo.chip(c) and topo.die(x) == topo.die(c))

    def server(H, h, role):
        i = HC[cls[H]].index(h)
        return dcs[cores[ranks_of[H][i // 2]]][2 * role + i % 2]

    C = topo.host(core)
    myb = [d for d, r in enumerate(ranks_of[C]) if core in dcs[cores[r]]][0]
    pos = dcs[cores[ranks_of[C][myb]]].index(core)
    role, is_rank = pos // 2, pos == 0
    head = HC[cls[C]][2 * myb + pos % 2]
    src_host = C if role == 0 else nb[C]["sw"]
    sr = ranks_of[src_host]
    sib = server(C, head, 1 - role)
    far = server(nb[C]["cb"], head, role)

    m_on = topo.mask(core, sib)
    m_off = topo.mask(core, far)
    offb = _bits(m_off)
    half = [_mask(offb[:len(offb) // 2]), _mask(offb[len(offb) // 2:])]
    quar = [_mask(offb[i * len(offb) // 4:(i + 1) * len(offb) // 4]) for i in range(4)]
    m_up = m_on & ~m_off
    upb = _bits(m_up)
    cnt = lambda m: len(_bits(m))

    te, ve, ac, sy, sem = g.tensor, g.vector, g.scalar, g.sync, T.sem
    nev, sent = [0], [0]
    Exp, MIN = ActivationFunctionType.Exp, AluOpType.min

    def ev():
        nev[0] += 1
        return sem["e%d" % (nev[0] - 1)]

    def tr(src, dst, dest, mask, rsem):
        rid, pid = topo.addr(dest, core)
        sent[0] += cnt(mask)
        return RemoteDMATransfer(dst_ids=[DstId(rid=rid, pnc=pid)], dma_engine_mask=mask, remote_sem=rsem,
                                 src=src, dst=dst)

    def send(trs):
        g.remote_dma_fused(trs, local_sem=sem.snt)

    eone, eidn = ev(), ev()
    if is_rank:
        ve.memset(T.ones[:], 1.0).then_inc(eone, 1)
    else:
        ezero = ev()
        ve.memset(T.ones[:], 0.0).then_inc(ezero, 1)
        ac.wait_ge(ezero, 1)
        ac.activation(T.ones[:], T.ones[:], Exp).then_inc(eone, 1)
    g.wait_ge(eone, 1)
    g.affine_select(T.idn[:], T.ones[:], [[-1, D]], AluOpType.is_equal, 0.0, 0, 1).then_inc(eidn, 1)

    m_big, m_sm = _mask(upb[:len(upb) // 2]), [_mask(upb[len(upb) // 2:3 * len(upb) // 4]), _mask(upb[3 * len(upb) // 4:])]
    if role == 1:
        pc_waits = [(sem.ow0, cnt(half[0])), (sem.ow1, cnt(half[0]))]
        own_waits = pc_waits + [(sem.oq, 2 * cnt(quar[0]))]
    elif is_rank:
        pc_waits = own_waits = [(sem.rpo, 3), (sem.ow1, cnt(m_big))]
    else:
        pc_waits = own_waits = [(sem.ow0, cnt(m_sm[0])), (sem.ow1, cnt(m_sm[0]))]
    Xh, Yh = HC[cls[C]], HC[1 - cls[C]]
    xlo, xhi, ylo, yhi = Xh[0] * D, (Xh[-1] + 1) * D, Yh[0] * D, (Yh[-1] + 1) * D
    if is_rank:
        other = cores[ranks_of[C][1 - myb]]
        sy.dma_start(T.vl[:, ylo:yhi], T.v[:, ylo:yhi]).then_inc(sem.ld, 16)
        ac.dma_start(T.kl[:, ylo:yhi], T.k[:, ylo:yhi]).then_inc(sem.ld, 16)
        sy.dma_start(T.ql[:, ylo:yhi], T.q[:, ylo:yhi]).then_inc(sem.ldq, 16)
        ac.dma_start(T.vl[:, xlo:xhi], T.v[:, xlo:xhi]).then_inc(sem.ld2, 16)
        sy.dma_start(T.kl[:, xlo:xhi], T.k[:, xlo:xhi]).then_inc(sem.ld2, 16)
        ac.dma_start(T.ql[:, xlo:xhi], T.q[:, xlo:xhi]).then_inc(sem.ld2, 16)
        oq, ok = (0, 2 * D) if myb == 0 else (2 * D, 0)
        okv = min(D, ok)

        def pack(h, out, o0, s, bufs):
            for buf, off in bufs:
                ve.tensor_copy(out[:, o0 + off:o0 + off + D], buf[:, h * D:(h + 1) * D]).then_inc(s, 1)
        ve.wait_ge(sem.ld, 32)
        nyh = len(Yh) // 2
        Y1, Y2 = Yh[myb * nyh:(myb + 1) * nyh], Yh[(1 - myb) * nyh:(2 - myb) * nyh]
        for hs_, s_ in ((Y1, sem.rpd), (Y2, sem.rpe)):
            for h in hs_:
                pack(h, T.x, h * PK, s_, ((T.vl, D), (T.kl, ok)))
        ve.wait_ge(sem.ld2, 48)
        full = ((T.ql, oq), (T.vl, D), (T.kl, ok))
        for h in Xh:
            if h != head:
                pack(h, T.x, h * PK, sem.rpx, full)
        pack(head, T.own, myb * PK, sem.rpo, full)

        B = nb[C]["sw"]
        for hs_, s_, d_ in ((Y1, sem.rpd, sem.ow0), (Y2, sem.rpe, sem.ow1)):
            g.wait_ge(s_, 2 * len(hs_))
            send([tr(T.x[:, h * PK + okv:h * PK + okv + 2 * D], T.own[:, myb * PK + okv:myb * PK + okv + 2 * D],
                     server(B, h, 1), half[i], d_) for i, h in enumerate(hs_)])
        g.wait_ge(sem.ldq, 16)
        send([tr(T.ql[:, h * D:(h + 1) * D], T.own[:, myb * PK + oq:myb * PK + oq + D],
                 server(B, h, 1), quar[i], sem.oq) for i, h in enumerate(Yh)])
        g.wait_ge(sem.rpx, 3 * (len(Xh) - 1))
        trs, sm = [], list(m_sm)
        for h in Xh:
            if h != head:
                a = server(C, h, 0)
                trs.append(tr(T.x[:, h * PK:(h + 1) * PK], T.own[:, myb * PK:(myb + 1) * PK], a,
                              m_big if a == other else sm.pop(0), sem.ow0 if a in dcs[core] else sem.ow1))
        send(trs)

    slot = hosts.index(src_host)
    pcs = (myb, 1 - myb)
    for n, p in enumerate(pcs):
        g.wait_ge(pc_waits[n][0], pc_waits[n][1])
        send([tr(T.own[:, D + p * 256:D + (p + 1) * 256], T.kv[:, slot * 512 + p * 256:slot * 512 + (p + 1) * 256],
                 far, m_off, sem["kc%d" % n])])
    send([tr(T.own[:, D:D + 512], T.kv[:, slot * 512:(slot + 1) * 512], sib, m_up, sem.ks)])
    order = ["own", "sw", "cb", "dg"] if role == 0 else ["sw", "own", "dg", "cb"]
    due = [own_waits, [(sem.ks, cnt(m_up))], [(sem.kc0, cnt(m_off)), (sem.kc1, cnt(m_off))],
           [(sem.kf0, cnt(m_on)), (sem.kf1, cnt(m_on))]]
    cslot = hosts.index(nb[C][order[2]])
    for n, p in enumerate(pcs):
        g.wait_ge(due[2][n][0], due[2][n][1])
        send([tr(T.kv[:, cslot * 512 + p * 256:cslot * 512 + (p + 1) * 256],
                 T.kv[:, cslot * 512 + p * 256:cslot * 512 + (p + 1) * 256], sib, m_on, sem["kf%d" % n])])

    SB = [[T.s00, T.s10], [T.s01, T.s11]]
    PT, O = [T.pt0, T.pt1], [T.o0, T.o1]
    q = [T.own[:, 0:D], T.own[:, 5 * D:6 * D]]
    ncol, nun = [0], [0]

    def col(n):
        ncol[0] += n
        return T.st[:, ncol[0] - n:ncol[0]]
    blk = lambda buf, gi, b, w: buf[:, (gi * 2 + b) * w:(gi * 2 + b + 1) * w]
    pcols = lambda buf, u: buf[:, (u[0] * 4 + u[2][0]) * 256:(u[0] * 4 + u[2][-1] + 1) * 256]
    sap = lambda u: SB[u[0]][u[1]][:, (u[2][0] % 2) * 256:(u[2][-1] % 2 + 1) * 256]

    def kvof(j):
        return (T.own, D) if j == 0 else (T.kv, hosts.index(nb[C][order[j]]) * 512)

    plan = [[0], [1], [2, 3]] if role == 0 else [[0, 1], [2, 3]]
    te.wait_ge(eidn, 1)
    eo_prev, l_ready, nm_prev, l_prev = None, [], None, None
    for gi, subs in enumerate(plan):
        hs = sorted({j // 2 for j in subs})
        nh = len(hs)
        units = [(b, h, [j for j in subs if j // 2 == h]) for b in (0, 1) for h in hs]
        nu = len(units)
        es, ep, et, ec = [[ev() for _ in units] for _ in range(4)]
        eo, ered = [ev(), ev()], [ev(), ev()]
        pbank = [PT[(nun[0] + ui) % 2] for ui in range(nu)]
        nun[0] += nu
        nsc = [0] * nu
        for j in subs:
            buf, c0 = kvof(j)
            if j >= 2:
                parts = [([due[j][n]], pcs[n] * D, D) for n in (0, 1)]
            else:
                parts = [(due[j], 0, 2 * D)]
            for waits, o, w in parts:
                for s_, v_ in waits:
                    te.wait_ge(s_, v_)
                for ui, u in enumerate(units):
                    if j in u[2]:
                        te.matmul(SB[u[0]][u[1]][:, (j % 2) * 256 + o:(j % 2) * 256 + o + w], q[u[0]],
                                  buf[:, c0 + D + o:c0 + D + o + w], True, True).then_inc(es[ui], 1)
                        nsc[ui] += 1
        nmg = col(2 * nh)
        nmn = nmg if (nh == 1 and gi == 0) else col(2)
        nmr = [None, None]
        for ui, u in enumerate(units):
            b, i = u[0], hs.index(u[1])
            ve.wait_ge(es[ui], nsc[ui])
            ve.tensor_reduce(nmg[:, b * nh + i:b * nh + i + 1], sap(u), AxisListType.X, AluOpType.max,
                             negate=True).then_inc(ered[b], 1)
        ve.wait_ge(ered[0], 1)
        ve.wait_ge(ered[1], 1)
        nmr = [(ered[0], 1), (ered[1], 1)]
        if gi > 0:
            enm, ed, eal, ers = ev(), ev(), ev(), [ev(), ev()]
            dd, al = col(2), col(2)
            ve.tensor_tensor(nmn, nm_prev, nmg, MIN).then_inc(enm, 1)
            ve.wait_ge(enm, 1)
            ve.tensor_tensor(dd, nmn, nm_prev, AluOpType.subtract).then_inc(ed, 1)
            nmr = [(enm, 1), (enm, 1)]
        lgc = col(2 * nh)
        for ui, u in enumerate(units):
            b, i = u[0], hs.index(u[1])
            ac.wait_ge(nmr[b][0], nmr[b][1])
            ac.activation(pcols(T.p, u), sap(u), Exp, bias=nmn[:, b:b + 1], scale=1.0,
                          accum_out=lgc[:, i * 2 + b:i * 2 + b + 1]).then_inc(ep[ui], 1)
            if gi > 0 and ui == 0:
                ac.wait_ge(ed, 1)
                ac.activation(al, dd, Exp).then_inc(eal, 1)
        if gi > 0:
            ve.wait_ge(eal, 1)
            for b in (0, 1):
                ve.wait_ge(eo_prev[b][0], eo_prev[b][1])
                ve.tensor_scalar(blk(T.oo, gi, b, D), O[b][:, 0:D], al[:, b:b + 1], None,
                                 AluOpType.mult).then_inc(ers[b], 1)
        nmm = [sum(2 * len(u[2]) for u in units if u[0] == b) + (1 if gi > 0 else 0) for b in (0, 1)]
        done = [0, 0]
        for step in range(nu + 1):
            if step < nu:
                u = units[step]
                te.wait_ge(ep[step], 1)
                for t in range(2 * len(u[2])):
                    te.transpose(pbank[step][:, t * D:(t + 1) * D], pcols(T.p, u)[:, t * D:(t + 1) * D],
                                 T.idn[:]).then_inc(et[step], 1)
                if gi > 0 and done[u[0]] == 0:
                    te.wait_ge(ers[u[0]], 1)
                    te.matmul(O[u[0]][:, 0:D], T.idn[:], blk(T.oo, gi, u[0], D), True, False).then_inc(eo[u[0]], 1)
                    done[u[0]] += 1
            if step > 0:
                u = units[step - 1]
                te.wait_ge(ec[step - 1], 1)
                for t in range(2 * len(u[2])):
                    buf, c0 = kvof(u[2][t // 2])
                    c0 += 0 if t % 2 == 0 else 3 * D
                    done[u[0]] += 1
                    te.matmul(O[u[0]][:, 0:D], pcols(T.pts, u)[:, t * D:(t + 1) * D], buf[:, c0:c0 + D],
                              done[u[0]] == 1, done[u[0]] == nmm[u[0]]).then_inc(eo[u[0]], 1)
        for ui, u in enumerate(units):
            ve.wait_ge(et[ui], 2 * len(u[2]))
            ve.tensor_copy(pcols(T.pts, u), pbank[ui][:, 0:256 * len(u[2])]).then_inc(ec[ui], 1)
        eo_prev = [(eo[b], nmm[b]) for b in (0, 1)]
        for e in ep:
            ve.wait_ge(e, 1)
        lsum = lgc
        if gi > 0:
            etmp, el, tmp, lnew = ev(), ev(), col(2), col(2)
            for s, v in l_ready:
                ve.wait_ge(s, v)
            ve.tensor_tensor(tmp, l_prev, al, AluOpType.mult).then_inc(etmp, 1)
            ve.wait_ge(etmp, 1)
            ve.tensor_tensor(lnew, tmp, lsum, AluOpType.add).then_inc(el, 1)
            lsum, l_ready = lnew, [(el, 1)]
        nm_prev, l_prev = nmn, lsum
    ycol = lambda h: T.yl[:, h * D:(h + 1) * D]
    outs = [T.yo[:, 0:D], T.yo[:, D:2 * D]]
    if is_rank:
        outs[myb] = ycol(head)
    rc = col(2)
    er, ey = ev(), [ev(), ev()]
    for s, v in l_ready:
        ve.wait_ge(s, v)
    ve.reciprocal(rc, l_prev).then_inc(er, 1)
    ve.wait_ge(er, 1)
    ve.wait_ge(eo_prev[0][0], eo_prev[0][1])
    ve.tensor_scalar(outs[0], O[0][:, 0:D], rc[:, 0:1], None, AluOpType.mult).then_inc(ey[0], 1)
    ac.wait_ge(er, 1)
    ac.wait_ge(eo_prev[1][0], eo_prev[1][1])
    ac.activation(outs[1], O[1][:, 0:D], ActivationFunctionType.Identity, scale=rc[:, 1:2]).then_inc(ey[1], 1)

    g.wait_ge(ey[0], 1)
    g.wait_ge(ey[1], 1)
    if is_rank:
        send([tr(outs[1 - myb], ycol(head), cores[sr[1 - myb]], m_on, sem.yx)])
    elif role == 0:
        send([tr(outs[i], ycol(head), cores[sr[i]], (m_off, m_up)[i], sem.yx) for i in (0, 1)])
    else:
        send([tr(outs[i], ycol(head), cores[sr[i]], half[i], sem.yy) for i in (0, 1)])
    g.wait_ge(sem.snt, sent[0])

    if is_rank:
        sy.wait_ge(ey[myb], 1)
        sy.wait_ge(sem.yx, cnt(m_on) + 2 * cnt(m_up))
        sy.dma_start(T.y[:, xlo:xhi], T.yl[:, xlo:xhi]).then_inc(sem.st, 16)
        ac.wait_ge(sem.yy, len(Yh) * cnt(half[0]))
        ac.dma_start(T.y[:, ylo:yhi], T.yl[:, ylo:yhi]).then_inc(sem.st2, 16)
        sy.wait_ge(sem.st, 16)
        ac.wait_ge(sem.st2, 16)
